import numpy as np
import ml_dtypes


def mxq(x, axis, fmt="e4m3"):
    dtype, down = {"e4m3": (ml_dtypes.float8_e4m3fn, 7), "e5m2": (ml_dtypes.float8_e5m2, 14)}[fmt]
    v = np.moveaxis(np.asarray(x, np.float32).astype(ml_dtypes.bfloat16).astype(np.float64), axis, -1)
    blocks = v.reshape(v.shape[:-1] + (-1, 32))
    amax = np.abs(blocks).max(-1, keepdims=True)
    byte = np.maximum(np.where(amax > 0, np.frexp(amax)[1] - 1 + 127, 0) - down, 1)
    scale = np.exp2(byte - 127.0)
    codes = (blocks / scale).astype(np.float32).astype(dtype).astype(np.float64)
    return np.moveaxis((codes * scale).reshape(v.shape), -1, axis)


WIDE = False


def mx_kscale(k):
    if not WIDE:
        return np.ones(k)
    levels = np.array([10, -10, 5, -5, 0])
    if k % 512:
        return np.exp2(np.random.permutation(np.resize(levels, k // 32))).repeat(32)
    a = np.empty((k // 512, 16))
    for p in range(k // 512):
        a[p, :8] = np.random.permutation(np.resize(levels, 8))
        for g in range(8):
            far = levels[np.abs(levels - a[p, g]) >= 10]
            a[p, g + 8] = far[np.random.randint(len(far))]
    return np.exp2(a.ravel()).repeat(32)


def f64(x):
    return np.asarray(x).astype(np.float64)


def striped(idx):
    return np.tile(np.asarray(idx).reshape(-1, 16).T, (8, 1)).astype(np.uint16)


def unstriped(offs):
    return offs[:16].T.reshape(-1).astype(np.int64)


E2M1 = np.array([0.0, 0.5, 1.0, 1.5, 2.0, 3.0, 4.0, 6.0, -0.0, -0.5, -1.0, -1.5, -2.0, -3.0, -4.0, -6.0])


def pack_weight(w, fmt):
    k, n = w.shape
    w = f64(np.asarray(w, np.float32).astype(ml_dtypes.bfloat16)).reshape(k // 32, 32, n)
    amax = np.abs(w).max(1)
    if fmt == "e4m3":
        byte = np.frexp(amax)[1] - 1 + 127 - 7
    else:
        mant, ex = np.frexp(amax / 6.0)
        byte = np.where(mant > 0.5, ex, ex - 1) + 127
    byte = np.clip(np.where(amax > 0, byte, 1), 1, 254)
    scaled = (w * np.exp2(127.0 - byte)[:, None, :]).reshape(k, n).astype(np.float32)
    by_word = np.ascontiguousarray(scaled.reshape(k // 512, 128, 4, n).transpose(0, 1, 3, 2))
    if fmt == "e4m3":
        words = by_word.astype(ml_dtypes.float8_e4m3fn).view(np.uint8)
    else:
        c = by_word.astype(ml_dtypes.float4_e2m1fn).view(np.uint8) & 0xF
        words = (c[..., 0::2] | (c[..., 1::2] << 4)).reshape(k // 512, 128, 2 * n)
    return np.ascontiguousarray(words), np.ascontiguousarray(byte.astype(np.uint8).reshape(k // 512, 16, n))


def unpack_weight(words, scales, fmt):
    g, _, n = scales.shape
    words = np.ascontiguousarray(words).reshape(g, 128, n, -1)
    if fmt == "e4m3":
        vals = words.view(ml_dtypes.float8_e4m3fn).astype(np.float64)
    else:
        nib = np.empty((g, 128, n, 4), np.uint8)
        nib[..., 0::2] = words & 0xF
        nib[..., 1::2] = words >> 4
        vals = E2M1[nib]
    vals = vals * np.repeat(np.exp2(scales.astype(np.float64) - 127.0), 8, axis=1)[..., None]
    return vals.transpose(0, 1, 3, 2).reshape(g * 512, n)


def bf(x):
    return np.asarray(x, np.float32).astype(ml_dtypes.bfloat16)


def planes(Y):
    r, m = Y.shape
    b = f64(bf(Y)).reshape(r // 32, 32, m)
    amax = np.abs(b).max(1)
    byte = np.clip(np.where(amax > 0, np.frexp(amax)[1] - 1 + 127 - 7, 1), 1, 254)
    codes = (b * np.exp2(127.0 - byte)[:, None, :]).reshape(r, m).astype(np.float32).astype(ml_dtypes.float8_e4m3fn).view(np.uint8)
    words = codes.reshape(r // 512, 128, 4, m).transpose(0, 1, 3, 2)
    return np.ascontiguousarray(words), np.ascontiguousarray(byte.astype(np.uint8).reshape(r // 512, 16, m))


D, T, I, J, U, Z, E, M = 512, 2048, 512, 256, 1024, 1024, 512, 1024


def setup_inputs():
    n = np.random.standard_normal
    idx = np.random.permutation(T)[:I]
    idx2 = np.random.permutation(U)[:J]
    idx3 = np.random.permutation(Z)[:J]
    idx4 = np.random.permutation(M)[:J]
    fd = mx_kscale(D)
    fi = mx_kscale(I)
    ti = np.ones(T)
    ti[idx] = fi
    keysp = pack_weight(n((D, T)) / fd[:, None], "e2m1")
    return {
        "keys_words": keysp[0],
        "keys_scales": keysp[1],
        "notes": (n((D, U)) * 1.0 / np.sqrt(D) * fd[:, None]).astype(np.float32),
        "users2": (n((D, Z)) * 1.0 / np.sqrt(D) * fd[:, None]).astype(np.float32),
        "rowf": (np.random.uniform(0.02, 0.08, (I, 1)) * fi[:, None]).astype(np.float32),
        "vals": (n((E, T)) / ti).astype(np.float32),
        "held": (n((E, M))).astype(np.float32),
        "hgain": np.tile(np.random.uniform(0.5, 2.0, M), (128, 1)).astype(np.float32),
        "offs": striped(idx),
        "offs2": striped(idx2),
        "offs3": striped(idx3),
        "offs4": striped(idx4),
    }


def reference(keys_words, keys_scales, notes, users2, rowf, vals, held, hgain, offs, offs2, offs3, offs4):
    idx = unstriped(offs)
    idx2 = unstriped(offs2)
    idx3 = unstriped(offs3)
    idx4 = unstriped(offs4)
    keysu = unpack_weight(keys_words, keys_scales, "e2m1")
    keysidxg = keysu[:, idx]
    notesidx2q = mxq(f64(notes)[:, idx2], 0, "e4m3")
    g1 = keysidxg.T @ notesidx2q
    users2idx3q = mxq(f64(users2)[:, idx3], 0, "e4m3")
    g2 = keysidxg.T @ users2idx3q
    g0 = np.maximum(g1, g2)
    gr1 = g0 * f64(rowf)
    vt1 = f64(vals)[:, idx].T
    vt1q = mxq(vt1, 0, "e4m3")
    gr1q = mxq(gr1, 0, "e4m3")
    o = vt1q.T @ gr1q
    y = f64(held)[:, idx4] + o * f64(hgain)[:1][:, idx4]
    words, scales = planes(y)
    return y, words, scales

from contextlib import ExitStack

import concourse.mybir as mybir
from concourse.masks import make_identity

D, T, I, J, U, Z, E, M = 512, 2048, 512, 256, 1024, 1024, 512, 1024
FLOPS = 2 * (2 * D * I * J + I * E * J)

F32 = mybir.dt.float32
BF16 = mybir.dt.bfloat16
I32 = mybir.dt.int32
U32 = mybir.dt.uint32
U16 = mybir.dt.uint16
U8 = mybir.dt.uint8
FP8X4 = mybir.dt.float8_e4m3fn_x4
FP4X4 = mybir.dt.float4_e2m1fn_x4
COPY = mybir.ActivationFunctionType.Copy
ADD = mybir.AluOpType.add
MULT = mybir.AluOpType.mult
MAX = mybir.AluOpType.max

P = 128
PACK = 4
HALF = J // 2


def interleave(nc, dst, src):
    nc.vector.tensor_copy(
        out=dst.rearrange("p (c i) t -> p c t i", i=4),
        in_=src.rearrange("p t (c i) -> p c t i", i=4),
    )


def tile_attend_tab_larger_merge_pl_kernel(
    tc, keys_words, keys_scales, notes, users2, rowf, vals, held, hgain, offs, offs2, offs3, offs4, out_0, out_1, out_2
):
    nc = tc.nc
    with ExitStack() as ctx:
        lists = ctx.enter_context(tc.tile_pool(name="lists", bufs=1))
        sb = ctx.enter_context(tc.tile_pool(name="sb", bufs=1))
        ps = ctx.enter_context(tc.psum_pool(name="ps", bufs=1))

        def planes_of(src):
            return src.rearrange("(p t) n -> p t n", t=PACK)

        tok_list = lists.tile([P, I // 16], U16, name="tok_list")
        note_list = lists.tile([P, J // 16], U16, name="note_list")
        user_list = lists.tile([P, J // 16], U16, name="user_list")
        held_list = lists.tile([P, J // 16], U16, name="held_list")

        note_pool = [sb.tile([P, 2 * U], F32, name=f"note_pool{u}") for u in range(2)]
        user_pool = [sb.tile([P, 2 * Z], F32, name=f"user_pool{u}") for u in range(2)]
        val_pool = [sb.tile([P, T], F32, name=f"val_pool{t}", tag=f"val{t}", align_bytes=64) for t in range(PACK)]
        held_pair = sb.tile([P, 2 * M], F32, name="held_pair")
        held_pool = [sb.tile([P, M], F32, name=f"held_pool{t}") for t in (2, 3)]
        key_word_pool = sb.tile([P, T], U16, name="key_word_pool")
        key_scale_pool = sb.tile([P, T], U8, name="key_scale_pool")
        gain_pool = sb.tile([P, M], F32, name="gain_pool")
        row_factor = sb.tile([P, PACK], F32, name="row_factor")
        ident = sb.tile([P, P], F32, name="ident")

        nc.gpsimd.memset(key_scale_pool[:].bitcast(I32), 0)
        nc.vector.memset(gain_pool[0 : P - 1, :], 0.0)

        def load_pair(tile, src, u):
            nc.sync.dma_start(tile[:], src.rearrange("(p u v) n -> p u (v n)", u=2, v=2)[:, u, :])

        nc.sync.dma_start(key_word_pool[:].bitcast(I32), keys_words[0].bitcast(I32))
        nc.sync.dma_start(tok_list[:], offs)
        load_pair(note_pool[0], notes, 0)
        nc.sync.dma_start(note_list[:], offs2)
        for q in range(4):
            nc.sync.dma_start(
                key_scale_pool[32 * q : 32 * q + 4, :].bitcast(I32), keys_scales[0, 4 * q : 4 * q + 4, :].bitcast(I32)
            )
        load_pair(note_pool[1], notes, 1)
        nc.sync.dma_start(held_list[:], offs4)
        nc.sync.dma_start(gain_pool[P - 1 : P, :], hgain[0:1, :])
        load_pair(user_pool[0], users2, 0)
        nc.sync.dma_start(user_list[:], offs3)
        load_pair(user_pool[1], users2, 1)
        nc.sync.dma_start(row_factor[:], rowf.rearrange("(p r) o -> p (r o)", r=PACK))
        for t in range(PACK):
            nc.sync.dma_start(val_pool[t][:], planes_of(vals)[:, t, :])
        load_pair(held_pair, held, 0)
        for t in (2, 3):
            nc.sync.dma_start(held_pool[t - 2][:], planes_of(held)[:, t, :])
        make_identity(nc, ident[:])

        def quantize(name, src, words, parts=1):
            codes = sb.tile([P, words], U32, name=name + "_codes", align_bytes=64)
            scales = sb.tile([P, words], U8, name=name + "_scales", align_bytes=64)
            w = words // parts
            for h in range(parts):
                nc.vector.quantize_mx(
                    out=codes[:, h * w : (h + 1) * w].bitcast(FP8X4),
                    scales=scales[:, h * w : (h + 1) * w],
                    in_=src[:, h * w * PACK : (h + 1) * w * PACK],
                )
            return codes, scales

        def gather_columns(name, pools, offsets):
            picked = sb.tile([P, PACK, J], F32, name=name + "_picked")
            for t in range(PACK):
                window = pools[t // 2][:, (t % 2) * U : (t % 2 + 1) * U].indirect(offsets[:])
                if t == PACK - 1:
                    nc.vector.tensor_copy(picked[:, t, :], window)
                else:
                    nc.scalar.activation(picked[:, t, :], window, COPY)
            woven = sb.tile([P, J, PACK], BF16, name=name + "_woven", align_bytes=64)
            for h in range(2):
                interleave(nc, woven[:, h * HALF : (h + 1) * HALF, :], picked[:, :, h * HALF : (h + 1) * HALF])
            return quantize(name, woven[:].rearrange("p j t -> p (j t)"), J, 2)

        key_picked = sb.tile([P, I], U16, name="key_picked")
        nc.vector.tensor_copy(key_picked[:], key_word_pool[:].indirect(tok_list[:]))
        key_words = sb.tile([P, PACK, P], U16, name="key_words", align_bytes=64)
        nc.vector.tensor_copy(key_words[:], key_picked[:].rearrange("p (s r) -> p r s", r=PACK))

        key_scales = sb.tile([P, PACK, P], U8, name="key_scales", align_bytes=64)
        nc.vector.tensor_copy(key_scales[:].rearrange("p r s -> p s r"), key_scale_pool[:].indirect(tok_list[:]))

        note_codes, note_scales = gather_columns("note", note_pool, note_list)

        gain_row = sb.tile([P, J], F32, name="gain_row")
        nc.scalar.activation(gain_row[:], gain_pool[:].indirect(held_list[:]), COPY)
        gain_turned = ps.tile([P, 2, P], F32, name="gain_turned", tag="o", bufs=2)
        for h in range(2):
            nc.tensor.transpose(gain_turned[:, h, :], gain_row[:, h * P : (h + 1) * P], ident[:])
        gain_col = sb.tile([P, 2], F32, name="gain_col")
        nc.vector.tensor_copy(gain_col[:], gain_turned[:, :, P - 1])
        gain_spread = ps.tile([P, 2, P], F32, name="gain_spread", tag="o", bufs=2)
        for h in range(2):
            nc.tensor.transpose(gain_spread[:, h, :], gain_col[:, h : h + 1].to_broadcast([P, P]), ident[:])
        gain = sb.tile([P, J], F32, name="gain")
        nc.vector.tensor_copy(gain[:], gain_spread[:].rearrange("p h j -> p (h j)"))

        def scores(name, codes, scales):
            banks = []
            for h in range(2):
                bank = ps.tile([P, PACK, HALF], F32, name=f"{name}_bank{h}")
                cols = slice(h * HALF, (h + 1) * HALF)
                for r in range(PACK):
                    nc.tensor.matmul_mx(
                        out=bank[:, r, :],
                        lhsT=key_words[:, r, :].bitcast(FP4X4),
                        lhsT_scale=key_scales[:, r, :],
                        rhs=codes[:, cols].bitcast(FP8X4),
                        rhs_scale=scales[:, cols],
                        start=True,
                        stop=True,
                    )
                banks.append(bank)
            return banks

        g1_banks = scores("g1", note_codes, note_scales)
        g1 = [sb.tile([P, HALF, PACK], F32, name=f"g1_{h}") for h in range(2)]
        for h in range(2):
            nc.vector.tensor_copy(g1[h][:], g1_banks[h][:].rearrange("p r j -> p j r"))

        user_codes, user_scales = gather_columns("user", user_pool, user_list)
        g2_banks = scores("g2", user_codes, user_scales)
        g0 = [sb.tile([P, HALF, PACK], F32, name=f"g0_{h}") for h in range(2)]
        gr1 = sb.tile([P, J, PACK], BF16, name="gr1", align_bytes=64)
        for h in range(2):
            nc.vector.tensor_tensor(g0[h][:], g2_banks[h][:].rearrange("p r j -> p j r"), g1[h][:], MAX)
        for h in range(2):
            nc.vector.tensor_tensor(
                gr1[:, h * HALF : (h + 1) * HALF, :],
                g0[h][:],
                row_factor[:].unsqueeze(1).to_broadcast([P, HALF, PACK]),
                MULT,
            )
        gr1_codes, gr1_scales = quantize("gr1", gr1[:].rearrange("p j r -> p (j r)"), J)

        def turn_values(t):
            val_picked = sb.tile([P, I], BF16, name=f"val_picked{t}")
            if t < PACK - 1:
                nc.scalar.activation(val_picked[:], val_pool[t][:].indirect(tok_list[:]), COPY)
            else:
                nc.scalar.activation(val_picked[:, : I // 2], val_pool[t][:].indirect(tok_list[:, : I // 32]), COPY)
                nc.vector.tensor_copy(val_picked[:, I // 2 :], val_pool[t][:].indirect(tok_list[:, I // 32 :]))
            pairs = val_picked[:].bitcast(F32)
            turned = ps.tile([P, 2, P], F32, name=f"turned{t}", tag="turn", bufs=2)
            for u in range(2):
                nc.tensor.transpose(turned[:, u, :], pairs[:, u : 2 * P : 2], ident[:])
            return turned

        def second_product(t, turned):
            vt1 = sb.tile([P, P * PACK], BF16, name=f"vt1_{t}", tag=f"val{t + 1}", align_bytes=64)
            nc.scalar.copy(vt1[:].bitcast(F32).rearrange("p (e u) -> p e u", u=2), turned[:].rearrange("p u e -> p e u"))
            vt1_codes, vt1_scales = quantize(f"vt1_{t}", vt1[:], P)
            o_bank = ps.tile([P, J], F32, name=f"o_bank{t}", tag="o", bufs=2)
            nc.tensor.matmul_mx(
                out=o_bank[:],
                lhsT=vt1_codes[:].bitcast(FP8X4),
                lhsT_scale=vt1_scales[:],
                rhs=gr1_codes[:].bitcast(FP8X4),
                rhs_scale=gr1_scales[:],
                start=True,
                stop=True,
            )
            og = sb.tile([P, J], F32, name=f"gained{t}")
            nc.vector.tensor_tensor(og[:], o_bank[:], gain[:], MULT)
            return og


        gained = []
        turned_next = turn_values(0)
        for t in range(PACK):
            turned_now = turned_next
            if t + 1 < PACK:
                turned_next = turn_values(t + 1)
            gained.append(second_product(t, turned_now))

        y = sb.tile([P, PACK, J], F32, name="y")
        y_woven = sb.tile([P, J, PACK], BF16, name="y_woven", align_bytes=64)
        held_picked = [sb.tile([P, J], F32, name=f"held_picked{t}") for t in (1, 2)]
        nc.scalar.activation(held_picked[0][:], held_pair[:, M:].indirect(held_list[:]), COPY)
        nc.scalar.activation(held_picked[1][:], held_pool[0][:].indirect(held_list[:]), COPY)
        nc.vector.tensor_tensor(y[:, 0, :], held_pair[:].indirect(held_list[:]), gained[0][:], ADD)
        for t in (1, 2):
            nc.vector.tensor_tensor(y[:, t, :], held_picked[t - 1][:], gained[t][:], ADD)
        for h in range(2):
            cols = slice(h * HALF, (h + 1) * HALF)
            entries = held_list[:, h * HALF // 16 : (h + 1) * HALF // 16]
            nc.vector.tensor_tensor(y[:, 3, cols], held_pool[1][:].indirect(entries), gained[3][:, cols], ADD)
        for t in range(PACK):
            nc.sync.dma_start(planes_of(out_0)[:, t, :], y[:, t, :])
        for h in range(2):
            interleave(nc, y_woven[:, h * HALF : (h + 1) * HALF, :], y[:, :, h * HALF : (h + 1) * HALF])
        y_codes, y_scales = quantize("y", y_woven[:].rearrange("p j t -> p (j t)"), J, 2)
        nc.sync.dma_start(out_1[0].rearrange("p c r -> p (c r)").bitcast(I32), y_codes[:].bitcast(I32))
        for q in range(4):
            eng = nc.scalar if q % 2 else nc.sync
            eng.dma_start(out_2[0, 4 * q : 4 * q + 4, :].bitcast(I32), y_scales[32 * q : 32 * q + 4, :].bitcast(I32))
